import numpy as np
import ml_dtypes


def mxq(x, axis, fmt="e4m3"):
    dtype, down = {"e4m3": (ml_dtypes.float8_e4m3fn, 7), "e5m2": (ml_dtypes.float8_e5m2, 14)}[fmt]
    v = np.moveaxis(np.asarray(x, np.float32).astype(ml_dtypes.bfloat16).astype(np.float64), axis, -1)
    blocks = v.reshape(v.shape[:-1] + (-1, 32))
    amax = np.abs(blocks).max(-1, keepdims=True)
    byte = np.maximum(np.where(amax > 0, np.frexp(amax)[1] - 1 + 127, 0) - down, 1)
    scale = np.exp2(byte - 127.0)
    codes = (blocks / scale).astype(np.float32).astype(dtype).astype(np.float64)
    return np.moveaxis((codes * scale).reshape(v.shape), -1, axis)


WIDE = False


def mx_kscale(k):
    if not WIDE:
        return np.ones(k)
    levels = np.array([10, -10, 5, -5, 0])
    if k % 512:
        return np.exp2(np.random.permutation(np.resize(levels, k // 32))).repeat(32)
    a = np.empty((k // 512, 16))
    for p in range(k // 512):
        a[p, :8] = np.random.permutation(np.resize(levels, 8))
        for g in range(8):
            far = levels[np.abs(levels - a[p, g]) >= 10]
            a[p, g + 8] = far[np.random.randint(len(far))]
    return np.exp2(a.ravel()).repeat(32)


def f64(x):
    return np.asarray(x).astype(np.float64)


def striped(idx):
    return np.tile(idx.reshape(-1, 16).T, (8, 1)).astype(np.uint16)


def unstriped(offs):
    return offs[:16].T.reshape(-1).astype(np.int64)


E2M1 = np.array([0.0, 0.5, 1.0, 1.5, 2.0, 3.0, 4.0, 6.0, -0.0, -0.5, -1.0, -1.5, -2.0, -3.0, -4.0, -6.0])


def pack_weight(w, fmt):
    k, n = w.shape
    w = f64(np.asarray(w, np.float32).astype(ml_dtypes.bfloat16)).reshape(k // 32, 32, n)
    amax = np.abs(w).max(1)
    if fmt == "e4m3":
        byte = np.frexp(amax)[1] - 1 + 127 - 7
    else:
        mant, ex = np.frexp(amax / 6.0)
        byte = np.where(mant > 0.5, ex, ex - 1) + 127
    byte = np.clip(np.where(amax > 0, byte, 1), 1, 254)
    scaled = (w * np.exp2(127.0 - byte)[:, None, :]).reshape(k, n).astype(np.float32)
    by_word = np.ascontiguousarray(scaled.reshape(k // 512, 128, 4, n).transpose(0, 1, 3, 2))
    if fmt == "e4m3":
        words = by_word.astype(ml_dtypes.float8_e4m3fn).view(np.uint8)
    else:
        c = by_word.astype(ml_dtypes.float4_e2m1fn).view(np.uint8) & 0xF
        words = (c[..., 0::2] | (c[..., 1::2] << 4)).reshape(k // 512, 128, 2 * n)
    return np.ascontiguousarray(words), np.ascontiguousarray(byte.astype(np.uint8).reshape(k // 512, 16, n))


def unpack_weight(words, scales, fmt):
    g, _, n = scales.shape
    words = np.ascontiguousarray(words).reshape(g, 128, n, -1)
    if fmt == "e4m3":
        vals = words.view(ml_dtypes.float8_e4m3fn).astype(np.float64)
    else:
        nib = np.empty((g, 128, n, 4), np.uint8)
        nib[..., 0::2] = words & 0xF
        nib[..., 1::2] = words >> 4
        vals = E2M1[nib]
    vals = vals * np.repeat(np.exp2(scales.astype(np.float64) - 127.0), 8, axis=1)[..., None]
    return vals.transpose(0, 1, 3, 2).reshape(g * 512, n)


def gelu(v):
    return 0.5 * v * (1.0 + np.tanh(np.sqrt(2.0 / np.pi) * (v + 0.044715 * v**3)))


def bf(x):
    return np.asarray(x, np.float32).astype(ml_dtypes.bfloat16)


def planes(Y):
    n, m = Y.shape
    b = f64(bf(Y)).reshape(n // 32, 32, m)
    amax = np.abs(b).max(1)
    byte = np.clip(np.where(amax > 0, np.frexp(amax)[1] - 1 + 127 - 7, 1), 1, 254)
    codes = (b * np.exp2(127.0 - byte)[:, None, :]).reshape(n, m).astype(np.float32).astype(ml_dtypes.float8_e4m3fn).view(np.uint8)
    words = codes.reshape(n // 512, 128, 4, m).transpose(0, 1, 3, 2)
    return np.ascontiguousarray(words), np.ascontiguousarray(byte.astype(np.uint8).reshape(n // 512, 16, m))


K, T, S, P, H, N = 1536, 4096, 1024, 512, 1024, 1024


def setup_inputs():
    n = np.random.standard_normal
    s = mx_kscale(K)[:, None]
    u = mx_kscale(H)[:, None]
    tab_words, tab_scales = pack_weight(n((K, T)) * s, "e4m3")
    w1 = 0.9 * n((K, H)) / np.sqrt(K) / s
    spread = np.exp(0.8 * n(N))[None, :]
    w4_words, w4_scales = pack_weight(n((H, N)) / np.sqrt(H) * spread / u, "e2m1")
    return {
        "tab_words": tab_words, "tab_scales": tab_scales,
        "offs": striped(np.random.permutation(T)[:S]),
        "pos1": striped(np.random.permutation(S)[:P]),
        "pos2": striped(np.random.permutation(S)[:P]),
        "w1": w1.astype(np.float32),
        "thr": n(H).astype(np.float32),
        "sharp": np.random.uniform(1, 3, H).astype(np.float32),
        "share": np.random.uniform(0.1, 0.5, H).astype(np.float32),
        "clash": (n((H, P)) * u).astype(np.float32),
        "base": np.random.uniform(0.3, 0.9, H).astype(np.float32),
        "w4_words": w4_words, "w4_scales": w4_scales,
    }


def reference(tab_words, tab_scales, offs, pos1, pos2, w1, thr, sharp, share, clash, base, w4_words, w4_scales):
    v = unpack_weight(tab_words, tab_scales, "e4m3")[:, unstriped(offs)]
    h = mxq(f64(w1), 0, "e4m3").T @ v
    a = 1.0 / (1.0 + np.exp(-(h[:, unstriped(pos1)] + f64(thr)[:, None])))
    top = h.max(axis=1)
    c = 1.0 / (1.0 + np.exp(-f64(sharp)[:, None] * (h[:, unstriped(pos2)] - f64(share)[:, None] * top[:, None])))
    z = f64(clash) * a / (f64(base)[:, None] + c)
    w4 = unpack_weight(w4_words, w4_scales, "e2m1")
    y = w4.T @ mxq(z, 0, "e4m3")
    words, scales = planes(y)
    return y, words, scales

@@ -1,0 +1,292 @@
+from contextlib import ExitStack
+
+import concourse.mybir as mybir
+
+K, T, S, PAIRS, H, N = 1536, 4096, 1024, 512, 1024, 1024
+FLOPS = 2 * K * H * S + 2 * H * N * PAIRS
+
+F32 = mybir.dt.float32
+BF16 = mybir.dt.bfloat16
+I32 = mybir.dt.int32
+U32 = mybir.dt.uint32
+U16 = mybir.dt.uint16
+U8 = mybir.dt.uint8
+FP8X4 = mybir.dt.float8_e4m3fn_x4
+FP4X4 = mybir.dt.float4_e2m1fn_x4
+ACT = mybir.ActivationFunctionType
+ALU = mybir.AluOpType
+
+P = 128
+PACK = 4
+K_PASS = P * PACK
+BANK = 512
+K_PASSES = K // K_PASS
+R_GROUPS = H // K_PASS
+N_GROUPS = N // K_PASS
+CHUNKS = ((0, 256), (256, 256))
+
+
+def tile_list_permit_conflict_features_kernel(
+    tc, tab_words, tab_scales, offs, pos1, pos2, w1, thr, sharp, share, clash, base, w4_words, w4_scales,
+    out_0, out_1, out_2,
+):
+    nc = tc.nc
+    with ExitStack() as ctx:
+        keep = ctx.enter_context(tc.tile_pool(name="keep", bufs=1))
+        ring = ctx.enter_context(tc.tile_pool(name="ring", bufs=1))
+        psum = ctx.enter_context(tc.psum_pool(name="psum", bufs=1))
+
+        def page(name, width=K_PASS):
+            return ring.tile([P, PACK, width], F32, name=name, tag="page", bufs=9, align_bytes=64)
+
+        def bank(i, name):
+            return psum.tile([P, BANK], F32, name=name, tag="bank%d" % i)
+
+        offs_sb = keep.tile([P, S // 16], U16, name="offs_sb")
+        pos1_sb = keep.tile([P, PAIRS // 16], U16, name="pos1_sb")
+        pos2_sb = keep.tile([P, PAIRS // 16], U16, name="pos2_sb")
+        tabw = [keep.tile([P, T], U32, name="tabw%d" % a, align_bytes=64) for a in range(K_PASSES)]
+        tabs = keep.tile([P, T], U8, name="tabs", align_bytes=64)
+        w4s_raw = keep.tile([P, R_GROUPS, N], U8, name="w4s_raw", align_bytes=64)
+        nc.vector.memset(tabs[:].bitcast(I32), 0)
+        nc.vector.memset(w4s_raw[:].rearrange("p a n -> p (a n)").bitcast(I32), 0)
+
+        w1_raw = {}
+
+        def load_w1(b, a):
+            w1_raw[b, a] = page("w1raw%d%d" % (b, a))
+            rows = w1[a * K_PASS : (a + 1) * K_PASS, b * K_PASS : (b + 1) * K_PASS]
+            nc.sync.dma_start(out=w1_raw[b, a][:], in_=rows.rearrange("(p j) c -> p j c", j=PACK))
+
+        for q in range(4):
+            nc.scalar.dma_start(
+                out=tabs[32 * q : 32 * q + 4 * K_PASSES, :].bitcast(I32),
+                in_=tab_scales[:, 4 * q : 4 * q + 4, :].bitcast(I32),
+            )
+        rowvec = {}
+        for name, vec in (("thr", thr), ("sharp", sharp), ("share", share), ("base", base)):
+            rowvec[name] = keep.tile([P, R_GROUPS * PACK], F32, name=name + "_sb")
+            nc.scalar.dma_start(
+                out=rowvec[name][:].rearrange("p (b t) -> p b t", t=PACK),
+                in_=vec.rearrange("(b p t) -> p b t", b=R_GROUPS, t=PACK),
+            )
+
+        nc.sync.dma_start(out=offs_sb[:], in_=offs)
+        for a in range(K_PASSES):
+            nc.sync.dma_start(
+                out=tabw[a][:].bitcast(I32), in_=tab_words[a].rearrange("p n t -> p (n t)").bitcast(I32)
+            )
+        for a in range(K_PASSES):
+            load_w1(0, a)
+        nc.sync.dma_start(out=pos1_sb[:], in_=pos1)
+        nc.sync.dma_start(out=pos2_sb[:], in_=pos2)
+        for a in range(K_PASSES):
+            load_w1(1, a)
+        clash_sb = []
+        for b in range(R_GROUPS):
+            clash_sb.append(page("clash%d" % b))
+            rows = clash[b * K_PASS : (b + 1) * K_PASS, :]
+            nc.sync.dma_start(out=clash_sb[b][:], in_=rows.rearrange("(p t) m -> p t m", t=PACK))
+        w4_raw = []
+        for b in range(R_GROUPS):
+            w4_raw.append(keep.tile([P, 2 * N], U8, name="w4raw%d" % b, align_bytes=64))
+            nc.sync.dma_start(out=w4_raw[b][:].bitcast(I32), in_=w4_words[b].bitcast(I32))
+        for q in range(4):
+            nc.sync.dma_start(
+                out=w4s_raw[32 * q : 32 * q + 4, :, :].bitcast(I32),
+                in_=w4_scales[:, 4 * q : 4 * q + 4, :].rearrange("a r n -> r a n").bitcast(I32),
+            )
+
+        vw = [keep.tile([P, S], U32, name="vw%d" % a, align_bytes=64) for a in range(K_PASSES)]
+        vs = keep.tile([P, S], U8, name="vs", align_bytes=64)
+        w1q, w1s = {}, {}
+
+        def prepare_w1(b, a, th, eng):
+            wbf = ring.tile([P, 2, P, PACK], BF16, name="w1bf", tag="w1bf", bufs=4, align_bytes=64)
+            src = w1_raw[b, a][:].rearrange("p j (m t) -> p m j t", t=PACK)[:, :, :, 2 * th : 2 * th + 2]
+            dst = wbf[:].rearrange("p t m j -> p m j t")
+            if eng == "scalar":
+                nc.scalar.copy(out=dst, in_=src)
+            else:
+                nc.vector.tensor_copy(out=dst, in_=src)
+            w1q[b, a, th] = keep.tile([P, 2 * P], U32, name="w1q%d%d%d" % (b, a, th), align_bytes=64)
+            w1s[b, a, th] = keep.tile([P, 2 * P], U8, name="w1s%d%d%d" % (b, a, th), align_bytes=64)
+            nc.vector.quantize_mx(
+                out=w1q[b, a, th][:].bitcast(FP8X4),
+                scales=w1s[b, a, th][:],
+                in_=wbf[:].rearrange("p t m j -> p (t m j)"),
+            )
+
+        def h_pass(acc, b, a, t):
+            cols = slice((t % 2) * P, (t % 2 + 1) * P)
+            for half in range(2):
+                js = slice(half * BANK, (half + 1) * BANK)
+                nc.tensor.matmul_mx(
+                    out=acc[half][:],
+                    lhsT=w1q[b, a, t // 2][:, cols].bitcast(FP8X4),
+                    lhsT_scale=w1s[b, a, t // 2][:, cols],
+                    rhs=vw[a][:, js].bitcast(FP8X4),
+                    rhs_scale=vs[4 * a : P, js],
+                    start=(a == 0),
+                    stop=(a == K_PASSES - 1),
+                )
+
+        neg_gain = keep.tile([P, R_GROUPS * PACK], F32, name="neg_gain")
+        nc.vector.scalar_tensor_tensor(
+            out=neg_gain[:], in0=rowvec["sharp"][:], scalar=-1.0, in1=rowvec["share"][:], op0=ALU.mult, op1=ALU.mult
+        )
+        tops = keep.tile([P, 2 * R_GROUPS * PACK], F32, name="tops")
+        gate_bias = keep.tile([P, R_GROUPS * PACK], F32, name="gate_bias")
+        a_sb = [page("a0"), None]
+        c_sb = [page("c0"), None]
+
+        def look(acc, b, t):
+            r = PACK * b + t
+            if r == R_GROUPS * PACK - 1:
+                h = ring.tile([P, S], F32, name="h_last", tag="h_last", bufs=1)
+            else:
+                h = ring.tile([P, S], F32, name="h", tag="h", bufs=4)
+            for half in range(2):
+                nc.vector.tensor_scalar(
+                    out=h[:, half * BANK : (half + 1) * BANK], in0=acc[half][:], scalar1=1.0, scalar2=None,
+                    op0=ALU.mult, op1=ALU.max, accum_out=tops[:, 2 * r + half : 2 * r + half + 1],
+                )
+            nc.vector.tensor_scalar(
+                out=gate_bias[:, r : r + 1], in0=tops[:, 2 * r : 2 * r + 1], scalar1=tops[:, 2 * r + 1 : 2 * r + 2],
+                scalar2=neg_gain[:, r : r + 1], op0=ALU.max, op1=ALU.mult,
+            )
+            nc.scalar.activation(
+                out=a_sb[b][:, t, :], in_=h[:].indirect(pos1_sb[:]), func=ACT.Sigmoid,
+                bias=rowvec["thr"][:, r : r + 1],
+            )
+            nc.scalar.activation(
+                out=c_sb[b][:, t, :], in_=h[:].indirect(pos2_sb[:]), func=ACT.Sigmoid,
+                bias=gate_bias[:, r : r + 1], scale=rowvec["sharp"][:, r : r + 1],
+            )
+
+        nc.vector.tensor_copy(out=vs[:], in_=tabs[:].indirect(offs_sb[:]))
+        acc0 = [[bank(2 * t + half, "h0%d%d" % (t, half)) for half in range(2)] for t in range(PACK)]
+        for a in range(K_PASSES):
+            nc.vector.tensor_copy(out=vw[a][:], in_=tabw[a][:].indirect(offs_sb[:]))
+        for a in range(K_PASSES):
+            prepare_w1(0, a, 0, "vector")
+            prepare_w1(0, a, 1, "scalar")
+            for t in range(PACK):
+                h_pass(acc0[t], 0, a, t)
+        a_sb[1] = page("a1")
+        c_sb[1] = page("c1")
+
+        def second_group(t):
+            acc = [bank(2 * t + half, "h1%d%d" % (t, half)) for half in range(2)]
+            for a in range(K_PASSES):
+                h_pass(acc, 1, a, t)
+            look(acc, 1, t)
+
+        look(acc0[0], 0, 0)
+        look(acc0[1], 0, 1)
+        prepare_w1(1, 0, 0, "vector")
+        look(acc0[2], 0, 2)
+        prepare_w1(1, 1, 0, "vector")
+        prepare_w1(1, 2, 0, "vector")
+        look(acc0[3], 0, 3)
+        second_group(0)
+        prepare_w1(1, 0, 1, "vector")
+        prepare_w1(1, 1, 1, "vector")
+        second_group(1)
+        prepare_w1(1, 2, 1, "vector")
+        second_group(2)
+        second_group(3)
+
+        w4p = []
+        for b in range(R_GROUPS):
+            w4p.append(keep.tile([P, 2 * N], U8, name="w4p%d" % b, align_bytes=64))
+            nc.vector.tensor_copy(
+                out=w4p[b][:].bitcast(U16).rearrange("p (g t q) -> p g t q", g=N_GROUPS, t=PACK),
+                in_=w4_raw[b][:].bitcast(U16).rearrange("p (g q t) -> p g t q", g=N_GROUPS, t=PACK),
+            )
+        w4s = keep.tile([P, R_GROUPS, N], U8, name="w4s", align_bytes=64)
+        nc.vector.tensor_copy(
+            out=w4s[:].rearrange("p a (g t q) -> p (a g) t q", g=N_GROUPS, t=PACK),
+            in_=w4s_raw[:].rearrange("p a (g q t) -> p (a g) t q", g=N_GROUPS, t=PACK),
+        )
+        for b in range(R_GROUPS):
+            for t in range(PACK):
+                nc.vector.tensor_tensor(
+                    out=a_sb[b][:, t, :], in0=a_sb[b][:, t, :], in1=clash_sb[b][:, t, :], op=ALU.mult
+                )
+
+        y_scales = keep.tile([P, N_GROUPS, PAIRS], U8, name="y_scales", align_bytes=64)
+        root = ring.tile([P, R_GROUPS * PACK * PAIRS], F32, name="root", tag="h_last", bufs=1)
+        accs = {}
+        for b in range(R_GROUPS):
+            for ci, (m0, mc) in enumerate(CHUNKS):
+                ms = slice(m0, m0 + mc)
+                r0 = PACK * (b * PAIRS + m0)
+                roots = root[:, r0 : r0 + PACK * mc]
+                for t in range(PACK):
+                    r = PACK * b + t
+                    nc.scalar.activation(
+                        out=roots[:, t * mc : (t + 1) * mc], in_=c_sb[b][:, t, ms], func=ACT.Abs_reciprocal_sqrt,
+                        bias=rowvec["base"][:, r : r + 1],
+                    )
+                part = ring.tile([P, PACK, mc], F32, name="part", tag="part", bufs=2)
+                roots3 = roots.rearrange("p (t m) -> p t m", t=PACK)
+                if b == 0 and ci == 0:
+                    nc.vector.tensor_tensor(out=part[:], in0=a_sb[b][:, :, ms], in1=roots3, op=ALU.mult)
+                    other = roots3
+                else:
+                    nc.scalar.activation(out=part[:], in_=roots3, func=ACT.Square)
+                    other = a_sb[b][:, :, ms]
+                zbf = ring.tile([P, mc * PACK], BF16, name="zbf", tag="bf", bufs=4, align_bytes=64)
+                nc.vector.tensor_tensor(
+                    out=zbf[:].rearrange("p (n i t) -> p n t i", i=2, t=PACK),
+                    in0=other.rearrange("p t (n i) -> p n t i", i=2),
+                    in1=part[:].rearrange("p t (n i) -> p n t i", i=2),
+                    op=ALU.mult,
+                )
+                zq = keep.tile([P, mc], U32, name="zq%d%d" % (ci, b), align_bytes=64)
+                zs = keep.tile([P, mc], U8, name="zs%d%d" % (ci, b), align_bytes=64)
+                nc.vector.quantize_mx(out=zq[:].bitcast(FP8X4), scales=zs[:], in_=zbf[:])
+                per_bank = BANK // mc
+                first_bank = R_GROUPS * PACK * m0 // BANK
+                for g in range(N_GROUPS):
+                    for t0 in range(0, PACK, per_bank):
+                        if b == 0:
+                            accs[ci, g, t0] = bank(first_bank + (g * PACK + t0) // per_bank, "y%d%d%d" % (ci, g, t0))
+                        acc = accs[ci, g, t0]
+                        for t in range(t0, t0 + per_bank):
+                            c0 = g * K_PASS + t * P
+                            nc.tensor.matmul_mx(
+                                out=acc[:, (t - t0) * mc : (t - t0 + 1) * mc],
+                                lhsT=w4p[b][:, 2 * c0 : 2 * (c0 + P)].bitcast(FP4X4),
+                                lhsT_scale=w4s[:, b, c0 : c0 + P],
+                                rhs=zq[:].bitcast(FP8X4),
+                                rhs_scale=zs[:],
+                                start=(b == 0 and t == t0),
+                                stop=(b == R_GROUPS - 1 and t == t0 + per_bank - 1),
+                            )
+        for ci, (m0, mc) in enumerate(CHUNKS):
+            ms = slice(m0, m0 + mc)
+            per_bank = BANK // mc
+            for g in range(N_GROUPS):
+                y = page("y%d%d" % (ci, g), mc)
+                for t0 in range(0, PACK, per_bank):
+                    nc.scalar.copy(
+                        out=y[:, t0 : t0 + per_bank, :].rearrange("p t m -> p (t m)"), in_=accs[ci, g, t0][:]
+                    )
+                rows = out_0[g * K_PASS : (g + 1) * K_PASS, ms]
+                nc.sync.dma_start(out=rows.rearrange("(p t) m -> p t m", t=PACK), in_=y[:])
+                ybf = ring.tile([P, mc * PACK], BF16, name="ybf", tag="bf", bufs=4, align_bytes=64)
+                nc.vector.tensor_copy(
+                    out=ybf[:].rearrange("p (n i t) -> p n t i", i=2, t=PACK),
+                    in_=y[:].rearrange("p t (n i) -> p n t i", i=2),
+                )
+                yq = keep.tile([P, mc], U32, name="yq%d%d" % (ci, g), align_bytes=64)
+                nc.vector.quantize_mx(out=yq[:].bitcast(FP8X4), scales=y_scales[:, g, ms], in_=ybf[:])
+                words = out_1[g].rearrange("p m t -> p (m t)")[:, PACK * m0 : PACK * (m0 + mc)]
+                nc.sync.dma_start(out=words.bitcast(I32), in_=yq[:].bitcast(I32))
+        for q in range(4):
+            (nc.scalar if q % 2 else nc.sync).dma_start(
+                out=out_2[:, 4 * q : 4 * q + 4, :].rearrange("g r m -> r g m").bitcast(I32),
+                in_=y_scales[32 * q : 32 * q + 4, :, :].bitcast(I32),
+            )

@@ -23,7 +23,7 @@ BANK = 512
 K_PASSES = K // K_PASS
 R_GROUPS = H // K_PASS
 N_GROUPS = N // K_PASS
-CHUNKS = ((0, 256), (256, 256))
+CHUNKS = ((0, 256), (256, 128), (384, 128))
 
 
 def tile_list_permit_conflict_features_kernel(
@@ -76,7 +76,9 @@ def tile_list_permit_conflict_features_kernel(
             nc.sync.dma_start(
                 out=tabw[a][:].bitcast(I32), in_=tab_words[a].rearrange("p n t -> p (n t)").bitcast(I32)
             )
-        for a in range(K_PASSES):
+            if a == 0:
+                load_w1(0, 0)
+        for a in range(1, K_PASSES):
             load_w1(0, a)
         nc.sync.dma_start(out=pos1_sb[:], in_=pos1)
         nc.sync.dma_start(out=pos2_sb[:], in_=pos2)
@@ -101,20 +103,24 @@ def tile_list_permit_conflict_features_kernel(
         vs = keep.tile([P, S], U8, name="vs", align_bytes=64)
         w1q, w1s = {}, {}
 
-        def prepare_w1(b, a, th, eng):
-            wbf = ring.tile([P, 2, P, PACK], BF16, name="w1bf", tag="w1bf", bufs=4, align_bytes=64)
+        w1bf = {}
+
+        def round_w1(b, a, th, eng="vector"):
+            w1bf[b, a, th] = ring.tile([P, 2, P, PACK], BF16, name="w1bf", tag="w1bf", bufs=4, align_bytes=64)
             src = w1_raw[b, a][:].rearrange("p j (m t) -> p m j t", t=PACK)[:, :, :, 2 * th : 2 * th + 2]
-            dst = wbf[:].rearrange("p t m j -> p m j t")
+            dst = w1bf[b, a, th][:].rearrange("p t m j -> p m j t")
             if eng == "scalar":
                 nc.scalar.copy(out=dst, in_=src)
             else:
                 nc.vector.tensor_copy(out=dst, in_=src)
+
+        def quantise_w1(b, a, th):
             w1q[b, a, th] = keep.tile([P, 2 * P], U32, name="w1q%d%d%d" % (b, a, th), align_bytes=64)
             w1s[b, a, th] = keep.tile([P, 2 * P], U8, name="w1s%d%d%d" % (b, a, th), align_bytes=64)
             nc.vector.quantize_mx(
                 out=w1q[b, a, th][:].bitcast(FP8X4),
                 scales=w1s[b, a, th][:],
-                in_=wbf[:].rearrange("p t m j -> p (t m j)"),
+                in_=w1bf[b, a, th][:].rearrange("p t m j -> p (t m j)"),
             )
 
         def h_pass(acc, b, a, t):
@@ -137,85 +143,135 @@ def tile_list_permit_conflict_features_kernel(
         )
         tops = keep.tile([P, 2 * R_GROUPS * PACK], F32, name="tops")
         gate_bias = keep.tile([P, R_GROUPS * PACK], F32, name="gate_bias")
-        a_sb = [page("a0"), None]
-        c_sb = [page("c0"), None]
+        a_sb = [page("a%d" % b) for b in range(R_GROUPS)]
+        c_sb = [page("c%d" % b) for b in range(R_GROUPS)]
+        h_acc, h_sb = {}, {}
 
-        def look(acc, b, t):
-            r = PACK * b + t
-            if r == R_GROUPS * PACK - 1:
-                h = ring.tile([P, S], F32, name="h_last", tag="h_last", bufs=1)
-            else:
-                h = ring.tile([P, S], F32, name="h", tag="h", bufs=4)
-            for half in range(2):
-                nc.vector.tensor_scalar(
-                    out=h[:, half * BANK : (half + 1) * BANK], in0=acc[half][:], scalar1=1.0, scalar2=None,
-                    op0=ALU.mult, op1=ALU.max, accum_out=tops[:, 2 * r + half : 2 * r + half + 1],
+        def open_tile(r):
+            h_acc[r] = [bank(2 * (r % PACK) + half, "h%d%d" % (r, half)) for half in range(2)]
+
+        def second_group(t):
+            open_tile(PACK + t)
+            for a in range(K_PASSES):
+                h_pass(h_acc[PACK + t], 1, a, t)
+
+        def leave_bank(r, half):
+            if half == 0:
+                if r == R_GROUPS * PACK - 1:
+                    h_sb[r] = ring.tile([P, S], F32, name="h_last", tag="h_last", bufs=1)
+                else:
+                    h_sb[r] = ring.tile([P, S], F32, name="h", tag="h", bufs=4)
+            nc.vector.tensor_scalar(
+                out=h_sb[r][:, half * BANK : (half + 1) * BANK], in0=h_acc[r][half][:], scalar1=1.0, scalar2=None,
+                op0=ALU.mult, op1=ALU.max, accum_out=tops[:, 2 * r + half : 2 * r + half + 1],
+            )
+            if half == 1:
+                nc.scalar.activation(
+                    out=a_sb[r // PACK][:, r % PACK, :], in_=h_sb[r][:].indirect(pos1_sb[:]), func=ACT.Sigmoid,
+                    bias=rowvec["thr"][:, r : r + 1],
                 )
+
+        def gate(r):
             nc.vector.tensor_scalar(
                 out=gate_bias[:, r : r + 1], in0=tops[:, 2 * r : 2 * r + 1], scalar1=tops[:, 2 * r + 1 : 2 * r + 2],
                 scalar2=neg_gain[:, r : r + 1], op0=ALU.max, op1=ALU.mult,
             )
             nc.scalar.activation(
-                out=a_sb[b][:, t, :], in_=h[:].indirect(pos1_sb[:]), func=ACT.Sigmoid,
-                bias=rowvec["thr"][:, r : r + 1],
-            )
-            nc.scalar.activation(
-                out=c_sb[b][:, t, :], in_=h[:].indirect(pos2_sb[:]), func=ACT.Sigmoid,
+                out=c_sb[r // PACK][:, r % PACK, :], in_=h_sb[r][:].indirect(pos2_sb[:]), func=ACT.Sigmoid,
                 bias=gate_bias[:, r : r + 1], scale=rowvec["sharp"][:, r : r + 1],
             )
 
-        nc.vector.tensor_copy(out=vs[:], in_=tabs[:].indirect(offs_sb[:]))
-        acc0 = [[bank(2 * t + half, "h0%d%d" % (t, half)) for half in range(2)] for t in range(PACK)]
-        for a in range(K_PASSES):
-            nc.vector.tensor_copy(out=vw[a][:], in_=tabw[a][:].indirect(offs_sb[:]))
-        for a in range(K_PASSES):
-            prepare_w1(0, a, 0, "vector")
-            prepare_w1(0, a, 1, "scalar")
-            for t in range(PACK):
-                h_pass(acc0[t], 0, a, t)
-        a_sb[1] = page("a1")
-        c_sb[1] = page("c1")
+        w4p = [keep.tile([P, 2 * N], U8, name="w4p%d" % b, align_bytes=64) for b in range(R_GROUPS)]
+        w4s = keep.tile([P, R_GROUPS, N], U8, name="w4s", align_bytes=64)
 
-        def second_group(t):
-            acc = [bank(2 * t + half, "h1%d%d" % (t, half)) for half in range(2)]
-            for a in range(K_PASSES):
-                h_pass(acc, 1, a, t)
-            look(acc, 1, t)
-
-        look(acc0[0], 0, 0)
-        look(acc0[1], 0, 1)
-        prepare_w1(1, 0, 0, "vector")
-        look(acc0[2], 0, 2)
-        prepare_w1(1, 1, 0, "vector")
-        prepare_w1(1, 2, 0, "vector")
-        look(acc0[3], 0, 3)
-        second_group(0)
-        prepare_w1(1, 0, 1, "vector")
-        prepare_w1(1, 1, 1, "vector")
-        second_group(1)
-        prepare_w1(1, 2, 1, "vector")
-        second_group(2)
-        second_group(3)
-
-        w4p = []
-        for b in range(R_GROUPS):
-            w4p.append(keep.tile([P, 2 * N], U8, name="w4p%d" % b, align_bytes=64))
+        def deal_w4_words(b):
             nc.vector.tensor_copy(
                 out=w4p[b][:].bitcast(U16).rearrange("p (g t q) -> p g t q", g=N_GROUPS, t=PACK),
                 in_=w4_raw[b][:].bitcast(U16).rearrange("p (g q t) -> p g t q", g=N_GROUPS, t=PACK),
             )
-        w4s = keep.tile([P, R_GROUPS, N], U8, name="w4s", align_bytes=64)
-        nc.vector.tensor_copy(
-            out=w4s[:].rearrange("p a (g t q) -> p (a g) t q", g=N_GROUPS, t=PACK),
-            in_=w4s_raw[:].rearrange("p a (g q t) -> p (a g) t q", g=N_GROUPS, t=PACK),
-        )
-        for b in range(R_GROUPS):
-            for t in range(PACK):
-                nc.vector.tensor_tensor(
-                    out=a_sb[b][:, t, :], in0=a_sb[b][:, t, :], in1=clash_sb[b][:, t, :], op=ALU.mult
-                )
+
+        def deal_w4_scales():
+            nc.vector.tensor_copy(
+                out=w4s[:].rearrange("p a (g t q) -> p (a g) t q", g=N_GROUPS, t=PACK),
+                in_=w4s_raw[:].rearrange("p a (g q t) -> p (a g) t q", g=N_GROUPS, t=PACK),
+            )
+
+        def weigh(b, ts):
+            nc.vector.tensor_tensor(out=a_sb[b][:, ts, :], in0=a_sb[b][:, ts, :], in1=clash_sb[b][:, ts, :], op=ALU.mult)
+
+        nc.vector.tensor_copy(out=vs[:], in_=tabs[:].indirect(offs_sb[:]))
+        for t in range(PACK):
+            open_tile(t)
+        nc.vector.tensor_copy(out=vw[0][:], in_=tabw[0][:].indirect(offs_sb[:]))
+        for th in range(2):
+            round_w1(0, 0, th, "scalar")
+            quantise_w1(0, 0, th)
+        for t in range(PACK):
+            h_pass(h_acc[t], 0, 0, t)
+        for a in range(1, K_PASSES):
+            nc.vector.tensor_copy(out=vw[a][:], in_=tabw[a][:].indirect(offs_sb[:]))
+        for a in range(1, K_PASSES):
+            round_w1(0, a, 0)
+            round_w1(0, a, 1, "scalar")
+            quantise_w1(0, a, 0)
+            for t in range(2):
+                h_pass(h_acc[t], 0, a, t)
+            if a == 1:
+                quantise_w1(0, a, 1)
+
+        leave_bank(0, 0)
+        leave_bank(0, 1)
+        quantise_w1(0, 2, 1)
+        for t in range(2, PACK):
+            for a in range(1, K_PASSES):
+                h_pass(h_acc[t], 0, a, t)
+        leave_bank(1, 0)
+        gate(0)
+        leave_bank(1, 1)
+        round_w1(1, 0, 0)
+        gate(1)
+        leave_bank(2, 0)
+        quantise_w1(1, 0, 0)
+        leave_bank(2, 1)
+        round_w1(1, 1, 0)
+        gate(2)
+        round_w1(1, 2, 0)
+        quantise_w1(1, 1, 0)
+        leave_bank(3, 0)
+        quantise_w1(1, 2, 0)
+        second_group(0)
+        second_group(1)
+        leave_bank(3, 1)
+        round_w1(1, 0, 1)
+        gate(3)
+        leave_bank(4, 0)
+        quantise_w1(1, 0, 1)
+        leave_bank(4, 1)
+        round_w1(1, 1, 1)
+        gate(4)
+        round_w1(1, 2, 1)
+        quantise_w1(1, 1, 1)
+        leave_bank(5, 0)
+        quantise_w1(1, 2, 1)
+        second_group(2)
+        second_group(3)
+        leave_bank(5, 1)
+        deal_w4_words(0)
+        gate(5)
+        leave_bank(6, 0)
+        leave_bank(6, 1)
+        deal_w4_words(1)
+        gate(6)
+        leave_bank(7, 0)
+        leave_bank(7, 1)
+        deal_w4_scales()
+        gate(7)
+        weigh(0, slice(0, PACK))
+        weigh(1, slice(0, 2))
+        weigh(1, slice(2, PACK))
 
         y_scales = keep.tile([P, N_GROUPS, PAIRS], U8, name="y_scales", align_bytes=64)
+        y_words = [keep.tile([P, PAIRS], U32, name="y_words%d" % g, align_bytes=64) for g in range(N_GROUPS)]
         root = ring.tile([P, R_GROUPS * PACK * PAIRS], F32, name="root", tag="h_last", bufs=1)
         accs = {}
         for b in range(R_GROUPS):
@@ -281,10 +337,10 @@ def tile_list_permit_conflict_features_kernel(
                     out=ybf[:].rearrange("p (n i t) -> p n t i", i=2, t=PACK),
                     in_=y[:].rearrange("p t (n i) -> p n t i", i=2),
                 )
-                yq = keep.tile([P, mc], U32, name="yq%d%d" % (ci, g), align_bytes=64)
-                nc.vector.quantize_mx(out=yq[:].bitcast(FP8X4), scales=y_scales[:, g, ms], in_=ybf[:])
-                words = out_1[g].rearrange("p m t -> p (m t)")[:, PACK * m0 : PACK * (m0 + mc)]
-                nc.sync.dma_start(out=words.bitcast(I32), in_=yq[:].bitcast(I32))
+                nc.vector.quantize_mx(out=y_words[g][:, ms].bitcast(FP8X4), scales=y_scales[:, g, ms], in_=ybf[:])
+                if m0 + mc == PAIRS:
+                    words = out_1[g].rearrange("p m t -> p (m t)")
+                    nc.sync.dma_start(out=words.bitcast(I32), in_=y_words[g][:].bitcast(I32))
         for q in range(4):
             (nc.scalar if q % 2 else nc.sync).dma_start(
                 out=out_2[:, 4 * q : 4 * q + 4, :].rearrange("g r m -> r g m").bitcast(I32),

@@ -18,12 +18,21 @@ ALU = mybir.AluOpType
 
 P = 128
 PACK = 4
-K_PASS = P * PACK
+PASS = P * PACK
 BANK = 512
-K_PASSES = K // K_PASS
-R_GROUPS = H // K_PASS
-N_GROUPS = N // K_PASS
-CHUNKS = ((0, 256), (256, 128), (384, 128))
+QUADRANTS = 4
+LIST_ROWS = 16
+K_PASSES = K // PASS
+R_GROUPS = H // PASS
+N_GROUPS = N // PASS
+ROW_TILES = R_GROUPS * PACK
+
+Y_CHUNKS = ((0, 256), (256, 128), (384, 128))
+Z_PIECES = ((0, 0, 256), (1, 0, 256), (0, 256, 256), (1, 256, 128), (1, 384, 128))
+
+PAGE_BUFS = 7
+H_BUFS = 4
+ROUNDED_BUFS = 4
 
 
 def tile_list_permit_conflict_features_kernel(
@@ -36,15 +45,18 @@ def tile_list_permit_conflict_features_kernel(
         ring = ctx.enter_context(tc.tile_pool(name="ring", bufs=1))
         psum = ctx.enter_context(tc.psum_pool(name="psum", bufs=1))
 
-        def page(name, width=K_PASS):
-            return ring.tile([P, PACK, width], F32, name=name, tag="page", bufs=9, align_bytes=64)
+        def page(name, width=PASS):
+            return ring.tile([P, PACK, width], F32, name=name, tag="page", bufs=PAGE_BUFS, align_bytes=64)
+
+        def late_page(name, i):
+            return ring.tile([P, PACK, PASS], F32, name=name, tag="late%d" % i, bufs=1, align_bytes=64)
 
         def bank(i, name):
             return psum.tile([P, BANK], F32, name=name, tag="bank%d" % i)
 
-        offs_sb = keep.tile([P, S // 16], U16, name="offs_sb")
-        pos1_sb = keep.tile([P, PAIRS // 16], U16, name="pos1_sb")
-        pos2_sb = keep.tile([P, PAIRS // 16], U16, name="pos2_sb")
+        offs_sb = keep.tile([P, S // LIST_ROWS], U16, name="offs_sb")
+        pos1_sb = keep.tile([P, PAIRS // LIST_ROWS], U16, name="pos1_sb")
+        pos2_sb = keep.tile([P, PAIRS // LIST_ROWS], U16, name="pos2_sb")
         tabw = [keep.tile([P, T], U32, name="tabw%d" % a, align_bytes=64) for a in range(K_PASSES)]
         tabs = keep.tile([P, T], U8, name="tabs", align_bytes=64)
         w4s_raw = keep.tile([P, R_GROUPS, N], U8, name="w4s_raw", align_bytes=64)
@@ -54,18 +66,21 @@ def tile_list_permit_conflict_features_kernel(
         w1_raw = {}
 
         def load_w1(b, a):
-            w1_raw[b, a] = page("w1raw%d%d" % (b, a))
-            rows = w1[a * K_PASS : (a + 1) * K_PASS, b * K_PASS : (b + 1) * K_PASS]
+            if b == 1 and a > 0:
+                w1_raw[b, a] = late_page("w1raw%d%d" % (b, a), a - 1)
+            else:
+                w1_raw[b, a] = page("w1raw%d%d" % (b, a))
+            rows = w1[a * PASS : (a + 1) * PASS, b * PASS : (b + 1) * PASS]
             nc.sync.dma_start(out=w1_raw[b, a][:], in_=rows.rearrange("(p j) c -> p j c", j=PACK))
 
-        for q in range(4):
+        for q in range(QUADRANTS):
             nc.scalar.dma_start(
                 out=tabs[32 * q : 32 * q + 4 * K_PASSES, :].bitcast(I32),
                 in_=tab_scales[:, 4 * q : 4 * q + 4, :].bitcast(I32),
             )
         rowvec = {}
         for name, vec in (("thr", thr), ("sharp", sharp), ("share", share), ("base", base)):
-            rowvec[name] = keep.tile([P, R_GROUPS * PACK], F32, name=name + "_sb")
+            rowvec[name] = keep.tile([P, ROW_TILES], F32, name=name + "_sb")
             nc.scalar.dma_start(
                 out=rowvec[name][:].rearrange("p (b t) -> p b t", t=PACK),
                 in_=vec.rearrange("(b p t) -> p b t", b=R_GROUPS, t=PACK),
@@ -76,59 +91,53 @@ def tile_list_permit_conflict_features_kernel(
             nc.sync.dma_start(
                 out=tabw[a][:].bitcast(I32), in_=tab_words[a].rearrange("p n t -> p (n t)").bitcast(I32)
             )
-            if a == 0:
-                load_w1(0, 0)
-        for a in range(1, K_PASSES):
             load_w1(0, a)
         nc.sync.dma_start(out=pos1_sb[:], in_=pos1)
         nc.sync.dma_start(out=pos2_sb[:], in_=pos2)
         for a in range(K_PASSES):
             load_w1(1, a)
-        clash_sb = []
-        for b in range(R_GROUPS):
-            clash_sb.append(page("clash%d" % b))
-            rows = clash[b * K_PASS : (b + 1) * K_PASS, :]
-            nc.sync.dma_start(out=clash_sb[b][:], in_=rows.rearrange("(p t) m -> p t m", t=PACK))
         w4_raw = []
         for b in range(R_GROUPS):
             w4_raw.append(keep.tile([P, 2 * N], U8, name="w4raw%d" % b, align_bytes=64))
             nc.sync.dma_start(out=w4_raw[b][:].bitcast(I32), in_=w4_words[b].bitcast(I32))
-        for q in range(4):
+        for q in range(QUADRANTS):
             nc.sync.dma_start(
                 out=w4s_raw[32 * q : 32 * q + 4, :, :].bitcast(I32),
-                in_=w4_scales[:, 4 * q : 4 * q + 4, :].rearrange("a r n -> r a n").bitcast(I32),
+                in_=w4_scales[:, 4 * q : 4 * q + 4, :].rearrange("a s n -> s a n").bitcast(I32),
             )
 
         vw = [keep.tile([P, S], U32, name="vw%d" % a, align_bytes=64) for a in range(K_PASSES)]
         vs = keep.tile([P, S], U8, name="vs", align_bytes=64)
-        w1q, w1s = {}, {}
+        w1bf, w1q, w1s = {}, {}, {}
 
-        w1bf = {}
+        def round_w1(engine_copy, b, a, pair):
+            w1bf[b, a, pair] = ring.tile(
+                [P, 2, P, PACK], BF16, name="w1bf", tag="w1bf", bufs=ROUNDED_BUFS, align_bytes=64
+            )
+            src = w1_raw[b, a][:].rearrange("p j (m t) -> p m j t", t=PACK)[:, :, :, 2 * pair : 2 * pair + 2]
+            engine_copy(out=w1bf[b, a, pair][:].rearrange("p t m j -> p m j t"), in_=src)
 
-        def round_w1(b, a, th, eng="vector"):
-            w1bf[b, a, th] = ring.tile([P, 2, P, PACK], BF16, name="w1bf", tag="w1bf", bufs=4, align_bytes=64)
-            src = w1_raw[b, a][:].rearrange("p j (m t) -> p m j t", t=PACK)[:, :, :, 2 * th : 2 * th + 2]
-            dst = w1bf[b, a, th][:].rearrange("p t m j -> p m j t")
-            if eng == "scalar":
-                nc.scalar.copy(out=dst, in_=src)
-            else:
-                nc.vector.tensor_copy(out=dst, in_=src)
-
-        def quantise_w1(b, a, th):
-            w1q[b, a, th] = keep.tile([P, 2 * P], U32, name="w1q%d%d%d" % (b, a, th), align_bytes=64)
-            w1s[b, a, th] = keep.tile([P, 2 * P], U8, name="w1s%d%d%d" % (b, a, th), align_bytes=64)
+        def quantise_w1(b, a, pair):
+            w1q[b, a, pair] = keep.tile([P, 2 * P], U32, name="w1q%d%d%d" % (b, a, pair), align_bytes=64)
+            w1s[b, a, pair] = keep.tile([P, 2 * P], U8, name="w1s%d%d%d" % (b, a, pair), align_bytes=64)
             nc.vector.quantize_mx(
-                out=w1q[b, a, th][:].bitcast(FP8X4),
-                scales=w1s[b, a, th][:],
-                in_=w1bf[b, a, th][:].rearrange("p t m j -> p (t m j)"),
+                out=w1q[b, a, pair][:].bitcast(FP8X4),
+                scales=w1s[b, a, pair][:],
+                in_=w1bf[b, a, pair][:].rearrange("p t m j -> p (t m j)"),
             )
 
-        def h_pass(acc, b, a, t):
+        h_acc, h_sb = {}, {}
+
+        def open_row_tile(r):
+            h_acc[r] = [bank(2 * (r % PACK) + half, "h%d%d" % (r, half)) for half in range(2)]
+
+        def h_pass(r, a):
+            b, t = divmod(r, PACK)
             cols = slice((t % 2) * P, (t % 2 + 1) * P)
             for half in range(2):
                 js = slice(half * BANK, (half + 1) * BANK)
                 nc.tensor.matmul_mx(
-                    out=acc[half][:],
+                    out=h_acc[r][half][:],
                     lhsT=w1q[b, a, t // 2][:, cols].bitcast(FP8X4),
                     lhsT_scale=w1s[b, a, t // 2][:, cols],
                     rhs=vw[a][:, js].bitcast(FP8X4),
@@ -137,30 +146,21 @@ def tile_list_permit_conflict_features_kernel(
                     stop=(a == K_PASSES - 1),
                 )
 
-        neg_gain = keep.tile([P, R_GROUPS * PACK], F32, name="neg_gain")
+        neg_gain = keep.tile([P, ROW_TILES], F32, name="neg_gain")
         nc.vector.scalar_tensor_tensor(
             out=neg_gain[:], in0=rowvec["sharp"][:], scalar=-1.0, in1=rowvec["share"][:], op0=ALU.mult, op1=ALU.mult
         )
-        tops = keep.tile([P, 2 * R_GROUPS * PACK], F32, name="tops")
-        gate_bias = keep.tile([P, R_GROUPS * PACK], F32, name="gate_bias")
+        tops = keep.tile([P, 2 * ROW_TILES], F32, name="tops")
+        gate_bias = keep.tile([P, ROW_TILES], F32, name="gate_bias")
         a_sb = [page("a%d" % b) for b in range(R_GROUPS)]
         c_sb = [page("c%d" % b) for b in range(R_GROUPS)]
-        h_acc, h_sb = {}, {}
-
-        def open_tile(r):
-            h_acc[r] = [bank(2 * (r % PACK) + half, "h%d%d" % (r, half)) for half in range(2)]
-
-        def second_group(t):
-            open_tile(PACK + t)
-            for a in range(K_PASSES):
-                h_pass(h_acc[PACK + t], 1, a, t)
 
         def leave_bank(r, half):
             if half == 0:
-                if r == R_GROUPS * PACK - 1:
+                if r == ROW_TILES - 1:
                     h_sb[r] = ring.tile([P, S], F32, name="h_last", tag="h_last", bufs=1)
                 else:
-                    h_sb[r] = ring.tile([P, S], F32, name="h", tag="h", bufs=4)
+                    h_sb[r] = ring.tile([P, S], F32, name="h", tag="h", bufs=H_BUFS)
             nc.vector.tensor_scalar(
                 out=h_sb[r][:, half * BANK : (half + 1) * BANK], in0=h_acc[r][half][:], scalar1=1.0, scalar2=None,
                 op0=ALU.mult, op1=ALU.max, accum_out=tops[:, 2 * r + half : 2 * r + half + 1],
@@ -171,7 +171,7 @@ def tile_list_permit_conflict_features_kernel(
                     bias=rowvec["thr"][:, r : r + 1],
                 )
 
-        def gate(r):
+        def second_look(r):
             nc.vector.tensor_scalar(
                 out=gate_bias[:, r : r + 1], in0=tops[:, 2 * r : 2 * r + 1], scalar1=tops[:, 2 * r + 1 : 2 * r + 2],
                 scalar2=neg_gain[:, r : r + 1], op0=ALU.max, op1=ALU.mult,
@@ -186,163 +186,159 @@ def tile_list_permit_conflict_features_kernel(
 
         def deal_w4_words(b):
             nc.vector.tensor_copy(
-                out=w4p[b][:].bitcast(U16).rearrange("p (g t q) -> p g t q", g=N_GROUPS, t=PACK),
-                in_=w4_raw[b][:].bitcast(U16).rearrange("p (g q t) -> p g t q", g=N_GROUPS, t=PACK),
+                out=w4p[b][:].bitcast(U16).rearrange("p (g t m) -> p g t m", g=N_GROUPS, t=PACK),
+                in_=w4_raw[b][:].bitcast(U16).rearrange("p (g m t) -> p g t m", g=N_GROUPS, t=PACK),
             )
 
-        def deal_w4_scales():
+        def deal_w4_planes():
             nc.vector.tensor_copy(
-                out=w4s[:].rearrange("p a (g t q) -> p (a g) t q", g=N_GROUPS, t=PACK),
-                in_=w4s_raw[:].rearrange("p a (g q t) -> p (a g) t q", g=N_GROUPS, t=PACK),
+                out=w4s[:].rearrange("p a (g t m) -> p (a g) t m", g=N_GROUPS, t=PACK),
+                in_=w4s_raw[:].rearrange("p a (g m t) -> p (a g) t m", g=N_GROUPS, t=PACK),
             )
 
-        def weigh(b, ts):
-            nc.vector.tensor_tensor(out=a_sb[b][:, ts, :], in0=a_sb[b][:, ts, :], in1=clash_sb[b][:, ts, :], op=ALU.mult)
+        def weigh(engine, b, ts):
+            engine.tensor_tensor(out=a_sb[b][:, ts, :], in0=a_sb[b][:, ts, :], in1=clash_sb[b][:, ts, :], op=ALU.mult)
 
         nc.vector.tensor_copy(out=vs[:], in_=tabs[:].indirect(offs_sb[:]))
-        for t in range(PACK):
-            open_tile(t)
-        nc.vector.tensor_copy(out=vw[0][:], in_=tabw[0][:].indirect(offs_sb[:]))
-        for th in range(2):
-            round_w1(0, 0, th, "scalar")
-            quantise_w1(0, 0, th)
-        for t in range(PACK):
-            h_pass(h_acc[t], 0, 0, t)
-        for a in range(1, K_PASSES):
+        for r in range(PACK):
+            open_row_tile(r)
+        last = K_PASSES - 1
+        for a in range(last):
             nc.vector.tensor_copy(out=vw[a][:], in_=tabw[a][:].indirect(offs_sb[:]))
-        for a in range(1, K_PASSES):
-            round_w1(0, a, 0)
-            round_w1(0, a, 1, "scalar")
-            quantise_w1(0, a, 0)
-            for t in range(2):
-                h_pass(h_acc[t], 0, a, t)
-            if a == 1:
-                quantise_w1(0, a, 1)
-
+            for pair in range(2):
+                round_w1(nc.scalar.copy, 0, a, pair)
+                quantise_w1(0, a, pair)
+            for r in range(PACK):
+                h_pass(r, a)
+        nc.vector.tensor_copy(out=vw[last][:], in_=tabw[last][:].indirect(offs_sb[:]))
+        round_w1(nc.vector.tensor_copy, 0, last, 0)
+        round_w1(nc.scalar.copy, 0, last, 1)
+        quantise_w1(0, last, 0)
+        h_pass(0, last)
+        h_pass(1, last)
         leave_bank(0, 0)
         leave_bank(0, 1)
-        quantise_w1(0, 2, 1)
-        for t in range(2, PACK):
-            for a in range(1, K_PASSES):
-                h_pass(h_acc[t], 0, a, t)
+        quantise_w1(0, last, 1)
+        h_pass(2, last)
+        h_pass(3, last)
         leave_bank(1, 0)
-        gate(0)
+        second_look(0)
         leave_bank(1, 1)
-        round_w1(1, 0, 0)
-        gate(1)
-        leave_bank(2, 0)
-        quantise_w1(1, 0, 0)
-        leave_bank(2, 1)
-        round_w1(1, 1, 0)
-        gate(2)
-        round_w1(1, 2, 0)
-        quantise_w1(1, 1, 0)
-        leave_bank(3, 0)
-        quantise_w1(1, 2, 0)
-        second_group(0)
-        second_group(1)
-        leave_bank(3, 1)
-        round_w1(1, 0, 1)
-        gate(3)
-        leave_bank(4, 0)
-        quantise_w1(1, 0, 1)
-        leave_bank(4, 1)
-        round_w1(1, 1, 1)
-        gate(4)
-        round_w1(1, 2, 1)
-        quantise_w1(1, 1, 1)
-        leave_bank(5, 0)
-        quantise_w1(1, 2, 1)
-        second_group(2)
-        second_group(3)
-        leave_bank(5, 1)
-        deal_w4_words(0)
-        gate(5)
-        leave_bank(6, 0)
-        leave_bank(6, 1)
-        deal_w4_words(1)
-        gate(6)
-        leave_bank(7, 0)
-        leave_bank(7, 1)
-        deal_w4_scales()
-        gate(7)
-        weigh(0, slice(0, PACK))
-        weigh(1, slice(0, 2))
-        weigh(1, slice(2, PACK))
+
+        for pair in range(2):
+            r = 2 * pair + 1
+            round_w1(nc.vector.tensor_copy, 1, 0, pair)
+            second_look(r)
+            leave_bank(r + 1, 0)
+            quantise_w1(1, 0, pair)
+            leave_bank(r + 1, 1)
+            round_w1(nc.vector.tensor_copy, 1, 1, pair)
+            second_look(r + 1)
+            round_w1(nc.vector.tensor_copy, 1, 2, pair)
+            quantise_w1(1, 1, pair)
+            leave_bank(r + 2, 0)
+            quantise_w1(1, 2, pair)
+            for ready in (PACK + 2 * pair, PACK + 2 * pair + 1):
+                open_row_tile(ready)
+                for a in range(K_PASSES):
+                    h_pass(ready, a)
+            leave_bank(r + 2, 1)
+        for b in range(R_GROUPS):
+            r = ROW_TILES - 3 + b
+            deal_w4_words(b)
+            second_look(r)
+            leave_bank(r + 1, 0)
+            leave_bank(r + 1, 1)
+        deal_w4_planes()
+        second_look(ROW_TILES - 1)
+
+        clash_sb = []
+        for b in range(R_GROUPS):
+            clash_sb.append(late_page("clash%d" % b, b))
+            rows = clash[b * PASS : (b + 1) * PASS, :]
+            nc.sync.dma_start(out=clash_sb[b][:], in_=rows.rearrange("(p t) m -> p t m", t=PACK))
+        for t in range(PACK):
+            weigh(nc.gpsimd, 0, slice(t, t + 1))
+        weigh(nc.vector, 1, slice(0, 2))
+        weigh(nc.vector, 1, slice(2, PACK))
 
         y_scales = keep.tile([P, N_GROUPS, PAIRS], U8, name="y_scales", align_bytes=64)
         y_words = [keep.tile([P, PAIRS], U32, name="y_words%d" % g, align_bytes=64) for g in range(N_GROUPS)]
-        root = ring.tile([P, R_GROUPS * PACK * PAIRS], F32, name="root", tag="h_last", bufs=1)
-        accs = {}
-        for b in range(R_GROUPS):
-            for ci, (m0, mc) in enumerate(CHUNKS):
-                ms = slice(m0, m0 + mc)
-                r0 = PACK * (b * PAIRS + m0)
-                roots = root[:, r0 : r0 + PACK * mc]
-                for t in range(PACK):
-                    r = PACK * b + t
-                    nc.scalar.activation(
-                        out=roots[:, t * mc : (t + 1) * mc], in_=c_sb[b][:, t, ms], func=ACT.Abs_reciprocal_sqrt,
-                        bias=rowvec["base"][:, r : r + 1],
-                    )
-                part = ring.tile([P, PACK, mc], F32, name="part", tag="part", bufs=2)
-                roots3 = roots.rearrange("p (t m) -> p t m", t=PACK)
-                if b == 0 and ci == 0:
-                    nc.vector.tensor_tensor(out=part[:], in0=a_sb[b][:, :, ms], in1=roots3, op=ALU.mult)
-                    other = roots3
-                else:
-                    nc.scalar.activation(out=part[:], in_=roots3, func=ACT.Square)
-                    other = a_sb[b][:, :, ms]
-                zbf = ring.tile([P, mc * PACK], BF16, name="zbf", tag="bf", bufs=4, align_bytes=64)
-                nc.vector.tensor_tensor(
-                    out=zbf[:].rearrange("p (n i t) -> p n t i", i=2, t=PACK),
-                    in0=other.rearrange("p t (n i) -> p n t i", i=2),
-                    in1=part[:].rearrange("p t (n i) -> p n t i", i=2),
-                    op=ALU.mult,
-                )
-                zq = keep.tile([P, mc], U32, name="zq%d%d" % (ci, b), align_bytes=64)
-                zs = keep.tile([P, mc], U8, name="zs%d%d" % (ci, b), align_bytes=64)
-                nc.vector.quantize_mx(out=zq[:].bitcast(FP8X4), scales=zs[:], in_=zbf[:])
-                per_bank = BANK // mc
-                first_bank = R_GROUPS * PACK * m0 // BANK
-                for g in range(N_GROUPS):
-                    for t0 in range(0, PACK, per_bank):
-                        if b == 0:
-                            accs[ci, g, t0] = bank(first_bank + (g * PACK + t0) // per_bank, "y%d%d%d" % (ci, g, t0))
-                        acc = accs[ci, g, t0]
-                        for t in range(t0, t0 + per_bank):
-                            c0 = g * K_PASS + t * P
-                            nc.tensor.matmul_mx(
-                                out=acc[:, (t - t0) * mc : (t - t0 + 1) * mc],
-                                lhsT=w4p[b][:, 2 * c0 : 2 * (c0 + P)].bitcast(FP4X4),
-                                lhsT_scale=w4s[:, b, c0 : c0 + P],
-                                rhs=zq[:].bitcast(FP8X4),
-                                rhs_scale=zs[:],
-                                start=(b == 0 and t == t0),
-                                stop=(b == R_GROUPS - 1 and t == t0 + per_bank - 1),
-                            )
-        for ci, (m0, mc) in enumerate(CHUNKS):
-            ms = slice(m0, m0 + mc)
-            per_bank = BANK // mc
+        inv_roots = ring.tile([P, ROW_TILES * PAIRS], F32, name="inv_roots", tag="h_last", bufs=1)
+        y_acc = {}
+
+        def y_passes(b, y0, yc, z_words, z_plane):
+            per_bank = BANK // yc
+            first_bank = N_GROUPS * PACK * y0 // BANK
             for g in range(N_GROUPS):
-                y = page("y%d%d" % (ci, g), mc)
+                for t0 in range(0, PACK, per_bank):
+                    if b == 0:
+                        y_acc[y0, g, t0] = bank(first_bank + (g * PACK + t0) // per_bank, "y%d_%d%d" % (y0, g, t0))
+                    for t in range(t0, t0 + per_bank):
+                        c0 = g * PASS + t * P
+                        nc.tensor.matmul_mx(
+                            out=y_acc[y0, g, t0][:, (t - t0) * yc : (t - t0 + 1) * yc],
+                            lhsT=w4p[b][:, 2 * c0 : 2 * (c0 + P)].bitcast(FP4X4),
+                            lhsT_scale=w4s[:, b, c0 : c0 + P],
+                            rhs=z_words.bitcast(FP8X4),
+                            rhs_scale=z_plane,
+                            start=(b == 0 and t == t0),
+                            stop=(b == R_GROUPS - 1 and t == t0 + per_bank - 1),
+                        )
+
+        def by_column_pairs(rows):
+            return rows.rearrange("p t (n i) -> p n t i", i=2)
+
+        def interleaved(flat):
+            return flat.rearrange("p (n i t) -> p n t i", i=2, t=PACK)
+
+        for piece, (b, m0, mc) in enumerate(Z_PIECES):
+            ms = slice(m0, m0 + mc)
+            first = PACK * (b * PAIRS + m0)
+            inv_root = inv_roots[:, first : first + PACK * mc].rearrange("p (t m) -> p t m", t=PACK)
+            for t in range(PACK):
+                r = PACK * b + t
+                nc.scalar.activation(
+                    out=inv_root[:, t, :], in_=c_sb[b][:, t, ms], func=ACT.Abs_reciprocal_sqrt,
+                    bias=rowvec["base"][:, r : r + 1],
+                )
+            partial = ring.tile([P, PACK, mc], F32, name="partial", tag="partial", bufs=2)
+            if piece == 0:
+                nc.vector.tensor_tensor(out=partial[:], in0=a_sb[b][:, :, ms], in1=inv_root, op=ALU.mult)
+                factor = inv_root
+            else:
+                nc.scalar.activation(out=partial[:], in_=inv_root, func=ACT.Square)
+                factor = a_sb[b][:, :, ms]
+            zbf = ring.tile([P, mc * PACK], BF16, name="zbf", tag="bf", bufs=ROUNDED_BUFS, align_bytes=64)
+            nc.vector.tensor_tensor(
+                out=interleaved(zbf[:]), in0=by_column_pairs(factor), in1=by_column_pairs(partial[:]), op=ALU.mult
+            )
+            zq = keep.tile([P, mc], U32, name="zq%d" % piece, align_bytes=64)
+            zs = keep.tile([P, mc], U8, name="zs%d" % piece, align_bytes=64)
+            nc.vector.quantize_mx(out=zq[:].bitcast(FP8X4), scales=zs[:], in_=zbf[:])
+            for y0, yc in Y_CHUNKS:
+                if m0 <= y0 < m0 + mc:
+                    y_passes(b, y0, yc, zq[:, y0 - m0 : y0 - m0 + yc], zs[:, y0 - m0 : y0 - m0 + yc])
+
+        for y0, yc in Y_CHUNKS:
+            ys = slice(y0, y0 + yc)
+            per_bank = BANK // yc
+            for g in range(N_GROUPS):
+                y = page("y%d_%d" % (y0, g), yc)
                 for t0 in range(0, PACK, per_bank):
                     nc.scalar.copy(
-                        out=y[:, t0 : t0 + per_bank, :].rearrange("p t m -> p (t m)"), in_=accs[ci, g, t0][:]
+                        out=y[:, t0 : t0 + per_bank, :].rearrange("p t m -> p (t m)"), in_=y_acc[y0, g, t0][:]
                     )
-                rows = out_0[g * K_PASS : (g + 1) * K_PASS, ms]
+                rows = out_0[g * PASS : (g + 1) * PASS, ys]
                 nc.sync.dma_start(out=rows.rearrange("(p t) m -> p t m", t=PACK), in_=y[:])
-                ybf = ring.tile([P, mc * PACK], BF16, name="ybf", tag="bf", bufs=4, align_bytes=64)
-                nc.vector.tensor_copy(
-                    out=ybf[:].rearrange("p (n i t) -> p n t i", i=2, t=PACK),
-                    in_=y[:].rearrange("p t (n i) -> p n t i", i=2),
-                )
-                nc.vector.quantize_mx(out=y_words[g][:, ms].bitcast(FP8X4), scales=y_scales[:, g, ms], in_=ybf[:])
-                if m0 + mc == PAIRS:
+                ybf = ring.tile([P, yc * PACK], BF16, name="ybf", tag="bf", bufs=ROUNDED_BUFS, align_bytes=64)
+                nc.vector.tensor_copy(out=interleaved(ybf[:]), in_=by_column_pairs(y[:]))
+                nc.vector.quantize_mx(out=y_words[g][:, ys].bitcast(FP8X4), scales=y_scales[:, g, ys], in_=ybf[:])
+                if y0 + yc == PAIRS:
                     words = out_1[g].rearrange("p m t -> p (m t)")
                     nc.sync.dma_start(out=words.bitcast(I32), in_=y_words[g][:].bitcast(I32))
-        for q in range(4):
+        for q in range(QUADRANTS):
             (nc.scalar if q % 2 else nc.sync).dma_start(
-                out=out_2[:, 4 * q : 4 * q + 4, :].rearrange("g r m -> r g m").bitcast(I32),
+                out=out_2[:, 4 * q : 4 * q + 4, :].rearrange("g s m -> s g m").bitcast(I32),
                 in_=y_scales[32 * q : 32 * q + 4, :, :].bitcast(I32),
             )

from contextlib import ExitStack

import concourse.mybir as mybir

K, T, S, PAIRS, H, N = 1536, 4096, 1024, 512, 1024, 1024
FLOPS = 2 * K * H * S + 2 * H * N * PAIRS

F32 = mybir.dt.float32
BF16 = mybir.dt.bfloat16
I32 = mybir.dt.int32
U32 = mybir.dt.uint32
U16 = mybir.dt.uint16
U8 = mybir.dt.uint8
FP8X4 = mybir.dt.float8_e4m3fn_x4
FP4X4 = mybir.dt.float4_e2m1fn_x4
ACT = mybir.ActivationFunctionType
ALU = mybir.AluOpType

P = 128
PACK = 4
PASS = P * PACK
BANK = 512
QUADRANTS = 4
LIST_ROWS = 16
K_PASSES = K // PASS
R_GROUPS = H // PASS
N_GROUPS = N // PASS
ROW_TILES = R_GROUPS * PACK

Y_CHUNKS = ((0, 256), (256, 128), (384, 128))
Z_PIECES = ((0, 0, 256), (1, 0, 256), (0, 256, 256), (1, 256, 128), (1, 384, 128))

PAGE_BUFS = 7
H_BUFS = 4
ROUNDED_BUFS = 4


def tile_list_permit_conflict_features_kernel(
    tc, tab_words, tab_scales, offs, pos1, pos2, w1, thr, sharp, share, clash, base, w4_words, w4_scales,
    out_0, out_1, out_2,
):
    nc = tc.nc
    with ExitStack() as ctx:
        keep = ctx.enter_context(tc.tile_pool(name="keep", bufs=1))
        ring = ctx.enter_context(tc.tile_pool(name="ring", bufs=1))
        psum = ctx.enter_context(tc.psum_pool(name="psum", bufs=1))

        def page(name, width=PASS):
            return ring.tile([P, PACK, width], F32, name=name, tag="page", bufs=PAGE_BUFS, align_bytes=64)

        def late_page(name, i):
            return ring.tile([P, PACK, PASS], F32, name=name, tag="late%d" % i, bufs=1, align_bytes=64)

        def bank(i, name):
            return psum.tile([P, BANK], F32, name=name, tag="bank%d" % i)

        offs_sb = keep.tile([P, S // LIST_ROWS], U16, name="offs_sb")
        pos1_sb = keep.tile([P, PAIRS // LIST_ROWS], U16, name="pos1_sb")
        pos2_sb = keep.tile([P, PAIRS // LIST_ROWS], U16, name="pos2_sb")
        tabw = [keep.tile([P, T], U32, name="tabw%d" % a, align_bytes=64) for a in range(K_PASSES)]
        tabs = keep.tile([P, T], U8, name="tabs", align_bytes=64)
        w4s_raw = keep.tile([P, R_GROUPS, N], U8, name="w4s_raw", align_bytes=64)
        nc.vector.memset(tabs[:].bitcast(I32), 0)
        nc.vector.memset(w4s_raw[:].rearrange("p a n -> p (a n)").bitcast(I32), 0)

        w1_raw = {}

        def load_w1(b, a):
            if b == 1 and a > 0:
                w1_raw[b, a] = late_page("w1raw%d%d" % (b, a), a - 1)
            else:
                w1_raw[b, a] = page("w1raw%d%d" % (b, a))
            rows = w1[a * PASS : (a + 1) * PASS, b * PASS : (b + 1) * PASS]
            nc.sync.dma_start(out=w1_raw[b, a][:], in_=rows.rearrange("(p j) c -> p j c", j=PACK))

        for q in range(QUADRANTS):
            nc.scalar.dma_start(
                out=tabs[32 * q : 32 * q + 4 * K_PASSES, :].bitcast(I32),
                in_=tab_scales[:, 4 * q : 4 * q + 4, :].bitcast(I32),
            )
        rowvec = {}
        for name, vec in (("thr", thr), ("sharp", sharp), ("share", share), ("base", base)):
            rowvec[name] = keep.tile([P, ROW_TILES], F32, name=name + "_sb")
            nc.scalar.dma_start(
                out=rowvec[name][:].rearrange("p (b t) -> p b t", t=PACK),
                in_=vec.rearrange("(b p t) -> p b t", b=R_GROUPS, t=PACK),
            )

        nc.sync.dma_start(out=offs_sb[:], in_=offs)
        for a in range(K_PASSES):
            nc.sync.dma_start(
                out=tabw[a][:].bitcast(I32), in_=tab_words[a].rearrange("p n t -> p (n t)").bitcast(I32)
            )
            load_w1(0, a)
        nc.sync.dma_start(out=pos1_sb[:], in_=pos1)
        nc.sync.dma_start(out=pos2_sb[:], in_=pos2)
        for a in range(K_PASSES):
            load_w1(1, a)
        w4_raw = []
        for b in range(R_GROUPS):
            w4_raw.append(keep.tile([P, 2 * N], U8, name="w4raw%d" % b, align_bytes=64))
            nc.sync.dma_start(out=w4_raw[b][:].bitcast(I32), in_=w4_words[b].bitcast(I32))
        for q in range(QUADRANTS):
            nc.sync.dma_start(
                out=w4s_raw[32 * q : 32 * q + 4, :, :].bitcast(I32),
                in_=w4_scales[:, 4 * q : 4 * q + 4, :].rearrange("a s n -> s a n").bitcast(I32),
            )

        vw = [keep.tile([P, S], U32, name="vw%d" % a, align_bytes=64) for a in range(K_PASSES)]
        vs = keep.tile([P, S], U8, name="vs", align_bytes=64)
        w1bf, w1q, w1s = {}, {}, {}

        def round_w1(engine_copy, b, a, pair):
            w1bf[b, a, pair] = ring.tile(
                [P, 2, P, PACK], BF16, name="w1bf", tag="w1bf", bufs=ROUNDED_BUFS, align_bytes=64
            )
            src = w1_raw[b, a][:].rearrange("p j (m t) -> p m j t", t=PACK)[:, :, :, 2 * pair : 2 * pair + 2]
            engine_copy(out=w1bf[b, a, pair][:].rearrange("p t m j -> p m j t"), in_=src)

        def quantise_w1(b, a, pair):
            w1q[b, a, pair] = keep.tile([P, 2 * P], U32, name="w1q%d%d%d" % (b, a, pair), align_bytes=64)
            w1s[b, a, pair] = keep.tile([P, 2 * P], U8, name="w1s%d%d%d" % (b, a, pair), align_bytes=64)
            nc.vector.quantize_mx(
                out=w1q[b, a, pair][:].bitcast(FP8X4),
                scales=w1s[b, a, pair][:],
                in_=w1bf[b, a, pair][:].rearrange("p t m j -> p (t m j)"),
            )

        h_acc, h_sb = {}, {}

        def open_row_tile(r):
            h_acc[r] = [bank(2 * (r % PACK) + half, "h%d%d" % (r, half)) for half in range(2)]

        def h_pass(r, a):
            b, t = divmod(r, PACK)
            cols = slice((t % 2) * P, (t % 2 + 1) * P)
            for half in range(2):
                js = slice(half * BANK, (half + 1) * BANK)
                nc.tensor.matmul_mx(
                    out=h_acc[r][half][:],
                    lhsT=w1q[b, a, t // 2][:, cols].bitcast(FP8X4),
                    lhsT_scale=w1s[b, a, t // 2][:, cols],
                    rhs=vw[a][:, js].bitcast(FP8X4),
                    rhs_scale=vs[4 * a : P, js],
                    start=(a == 0),
                    stop=(a == K_PASSES - 1),
                )

        neg_gain = keep.tile([P, ROW_TILES], F32, name="neg_gain")
        nc.vector.scalar_tensor_tensor(
            out=neg_gain[:], in0=rowvec["sharp"][:], scalar=-1.0, in1=rowvec["share"][:], op0=ALU.mult, op1=ALU.mult
        )
        tops = keep.tile([P, 2 * ROW_TILES], F32, name="tops")
        gate_bias = keep.tile([P, ROW_TILES], F32, name="gate_bias")
        a_sb = [page("a%d" % b) for b in range(R_GROUPS)]
        c_sb = [page("c%d" % b) for b in range(R_GROUPS)]

        def leave_bank(r, half):
            if half == 0:
                if r == ROW_TILES - 1:
                    h_sb[r] = ring.tile([P, S], F32, name="h_last", tag="h_last", bufs=1)
                else:
                    h_sb[r] = ring.tile([P, S], F32, name="h", tag="h", bufs=H_BUFS)
            nc.vector.tensor_scalar(
                out=h_sb[r][:, half * BANK : (half + 1) * BANK], in0=h_acc[r][half][:], scalar1=1.0, scalar2=None,
                op0=ALU.mult, op1=ALU.max, accum_out=tops[:, 2 * r + half : 2 * r + half + 1],
            )
            if half == 1:
                nc.scalar.activation(
                    out=a_sb[r // PACK][:, r % PACK, :], in_=h_sb[r][:].indirect(pos1_sb[:]), func=ACT.Sigmoid,
                    bias=rowvec["thr"][:, r : r + 1],
                )

        def second_look(r):
            nc.vector.tensor_scalar(
                out=gate_bias[:, r : r + 1], in0=tops[:, 2 * r : 2 * r + 1], scalar1=tops[:, 2 * r + 1 : 2 * r + 2],
                scalar2=neg_gain[:, r : r + 1], op0=ALU.max, op1=ALU.mult,
            )
            nc.scalar.activation(
                out=c_sb[r // PACK][:, r % PACK, :], in_=h_sb[r][:].indirect(pos2_sb[:]), func=ACT.Sigmoid,
                bias=gate_bias[:, r : r + 1], scale=rowvec["sharp"][:, r : r + 1],
            )

        w4p = [keep.tile([P, 2 * N], U8, name="w4p%d" % b, align_bytes=64) for b in range(R_GROUPS)]
        w4s = keep.tile([P, R_GROUPS, N], U8, name="w4s", align_bytes=64)

        def deal_w4_words(b):
            nc.vector.tensor_copy(
                out=w4p[b][:].bitcast(U16).rearrange("p (g t m) -> p g t m", g=N_GROUPS, t=PACK),
                in_=w4_raw[b][:].bitcast(U16).rearrange("p (g m t) -> p g t m", g=N_GROUPS, t=PACK),
            )

        def deal_w4_planes():
            nc.vector.tensor_copy(
                out=w4s[:].rearrange("p a (g t m) -> p (a g) t m", g=N_GROUPS, t=PACK),
                in_=w4s_raw[:].rearrange("p a (g m t) -> p (a g) t m", g=N_GROUPS, t=PACK),
            )

        def weigh(engine, b, ts):
            engine.tensor_tensor(out=a_sb[b][:, ts, :], in0=a_sb[b][:, ts, :], in1=clash_sb[b][:, ts, :], op=ALU.mult)

        nc.vector.tensor_copy(out=vs[:], in_=tabs[:].indirect(offs_sb[:]))
        for r in range(PACK):
            open_row_tile(r)
        last = K_PASSES - 1
        for a in range(last):
            nc.vector.tensor_copy(out=vw[a][:], in_=tabw[a][:].indirect(offs_sb[:]))
            for pair in range(2):
                round_w1(nc.scalar.copy, 0, a, pair)
                quantise_w1(0, a, pair)
            for r in range(PACK):
                h_pass(r, a)
        nc.vector.tensor_copy(out=vw[last][:], in_=tabw[last][:].indirect(offs_sb[:]))
        round_w1(nc.vector.tensor_copy, 0, last, 0)
        round_w1(nc.scalar.copy, 0, last, 1)
        quantise_w1(0, last, 0)
        h_pass(0, last)
        h_pass(1, last)
        leave_bank(0, 0)
        leave_bank(0, 1)
        quantise_w1(0, last, 1)
        h_pass(2, last)
        h_pass(3, last)
        leave_bank(1, 0)
        second_look(0)
        leave_bank(1, 1)

        for pair in range(2):
            r = 2 * pair + 1
            round_w1(nc.vector.tensor_copy, 1, 0, pair)
            second_look(r)
            leave_bank(r + 1, 0)
            quantise_w1(1, 0, pair)
            leave_bank(r + 1, 1)
            round_w1(nc.vector.tensor_copy, 1, 1, pair)
            second_look(r + 1)
            round_w1(nc.vector.tensor_copy, 1, 2, pair)
            quantise_w1(1, 1, pair)
            leave_bank(r + 2, 0)
            quantise_w1(1, 2, pair)
            for ready in (PACK + 2 * pair, PACK + 2 * pair + 1):
                open_row_tile(ready)
                for a in range(K_PASSES):
                    h_pass(ready, a)
            leave_bank(r + 2, 1)
        for b in range(R_GROUPS):
            r = ROW_TILES - 3 + b
            deal_w4_words(b)
            second_look(r)
            leave_bank(r + 1, 0)
            leave_bank(r + 1, 1)
        deal_w4_planes()
        second_look(ROW_TILES - 1)

        clash_sb = []
        for b in range(R_GROUPS):
            clash_sb.append(late_page("clash%d" % b, b))
            rows = clash[b * PASS : (b + 1) * PASS, :]
            nc.sync.dma_start(out=clash_sb[b][:], in_=rows.rearrange("(p t) m -> p t m", t=PACK))
        for t in range(PACK):
            weigh(nc.gpsimd, 0, slice(t, t + 1))
        weigh(nc.vector, 1, slice(0, 2))
        weigh(nc.vector, 1, slice(2, PACK))

        y_scales = keep.tile([P, N_GROUPS, PAIRS], U8, name="y_scales", align_bytes=64)
        y_words = [keep.tile([P, PAIRS], U32, name="y_words%d" % g, align_bytes=64) for g in range(N_GROUPS)]
        inv_roots = ring.tile([P, ROW_TILES * PAIRS], F32, name="inv_roots", tag="h_last", bufs=1)
        y_acc = {}

        def y_passes(b, y0, yc, z_words, z_plane):
            per_bank = BANK // yc
            first_bank = N_GROUPS * PACK * y0 // BANK
            for g in range(N_GROUPS):
                for t0 in range(0, PACK, per_bank):
                    if b == 0:
                        y_acc[y0, g, t0] = bank(first_bank + (g * PACK + t0) // per_bank, "y%d_%d%d" % (y0, g, t0))
                    for t in range(t0, t0 + per_bank):
                        c0 = g * PASS + t * P
                        nc.tensor.matmul_mx(
                            out=y_acc[y0, g, t0][:, (t - t0) * yc : (t - t0 + 1) * yc],
                            lhsT=w4p[b][:, 2 * c0 : 2 * (c0 + P)].bitcast(FP4X4),
                            lhsT_scale=w4s[:, b, c0 : c0 + P],
                            rhs=z_words.bitcast(FP8X4),
                            rhs_scale=z_plane,
                            start=(b == 0 and t == t0),
                            stop=(b == R_GROUPS - 1 and t == t0 + per_bank - 1),
                        )

        def by_column_pairs(rows):
            return rows.rearrange("p t (n i) -> p n t i", i=2)

        def interleaved(flat):
            return flat.rearrange("p (n i t) -> p n t i", i=2, t=PACK)

        for piece, (b, m0, mc) in enumerate(Z_PIECES):
            ms = slice(m0, m0 + mc)
            first = PACK * (b * PAIRS + m0)
            inv_root = inv_roots[:, first : first + PACK * mc].rearrange("p (t m) -> p t m", t=PACK)
            for t in range(PACK):
                r = PACK * b + t
                nc.scalar.activation(
                    out=inv_root[:, t, :], in_=c_sb[b][:, t, ms], func=ACT.Abs_reciprocal_sqrt,
                    bias=rowvec["base"][:, r : r + 1],
                )
            partial = ring.tile([P, PACK, mc], F32, name="partial", tag="partial", bufs=2)
            if piece == 0:
                nc.vector.tensor_tensor(out=partial[:], in0=a_sb[b][:, :, ms], in1=inv_root, op=ALU.mult)
                factor = inv_root
            else:
                nc.scalar.activation(out=partial[:], in_=inv_root, func=ACT.Square)
                factor = a_sb[b][:, :, ms]
            zbf = ring.tile([P, mc * PACK], BF16, name="zbf", tag="bf", bufs=ROUNDED_BUFS, align_bytes=64)
            nc.vector.tensor_tensor(
                out=interleaved(zbf[:]), in0=by_column_pairs(factor), in1=by_column_pairs(partial[:]), op=ALU.mult
            )
            zq = keep.tile([P, mc], U32, name="zq%d" % piece, align_bytes=64)
            zs = keep.tile([P, mc], U8, name="zs%d" % piece, align_bytes=64)
            nc.vector.quantize_mx(out=zq[:].bitcast(FP8X4), scales=zs[:], in_=zbf[:])
            for y0, yc in Y_CHUNKS:
                if m0 <= y0 < m0 + mc:
                    y_passes(b, y0, yc, zq[:, y0 - m0 : y0 - m0 + yc], zs[:, y0 - m0 : y0 - m0 + yc])

        for y0, yc in Y_CHUNKS:
            ys = slice(y0, y0 + yc)
            per_bank = BANK // yc
            for g in range(N_GROUPS):
                y = page("y%d_%d" % (y0, g), yc)
                for t0 in range(0, PACK, per_bank):
                    nc.scalar.copy(
                        out=y[:, t0 : t0 + per_bank, :].rearrange("p t m -> p (t m)"), in_=y_acc[y0, g, t0][:]
                    )
                rows = out_0[g * PASS : (g + 1) * PASS, ys]
                nc.sync.dma_start(out=rows.rearrange("(p t) m -> p t m", t=PACK), in_=y[:])
                ybf = ring.tile([P, yc * PACK], BF16, name="ybf", tag="bf", bufs=ROUNDED_BUFS, align_bytes=64)
                nc.vector.tensor_copy(out=interleaved(ybf[:]), in_=by_column_pairs(y[:]))
                nc.vector.quantize_mx(out=y_words[g][:, ys].bitcast(FP8X4), scales=y_scales[:, g, ys], in_=ybf[:])
                if y0 + yc == PAIRS:
                    words = out_1[g].rearrange("p m t -> p (m t)")
                    nc.sync.dma_start(out=words.bitcast(I32), in_=y_words[g][:].bitcast(I32))
        for q in range(QUADRANTS):
            (nc.scalar if q % 2 else nc.sync).dma_start(
                out=out_2[:, 4 * q : 4 * q + 4, :].rearrange("g s m -> s g m").bitcast(I32),
                in_=y_scales[32 * q : 32 * q + 4, :, :].bitcast(I32),
            )
